import numpy as np
import ml_dtypes


def mxq(x, axis, fmt="e4m3"):
    dtype, down = {"e4m3": (ml_dtypes.float8_e4m3fn, 7), "e5m2": (ml_dtypes.float8_e5m2, 14)}[fmt]
    v = np.moveaxis(np.asarray(x, np.float32).astype(ml_dtypes.bfloat16).astype(np.float64), axis, -1)
    blocks = v.reshape(v.shape[:-1] + (-1, 32))
    amax = np.abs(blocks).max(-1, keepdims=True)
    byte = np.maximum(np.where(amax > 0, np.frexp(amax)[1] - 1 + 127, 0) - down, 1)
    scale = np.exp2(byte - 127.0)
    codes = (blocks / scale).astype(np.float32).astype(dtype).astype(np.float64)
    return np.moveaxis((codes * scale).reshape(v.shape), -1, axis)


WIDE = False


def mx_kscale(k):
    if not WIDE:
        return np.ones(k)
    levels = np.array([10, -10, 5, -5, 0])
    if k % 512:
        return np.exp2(np.random.permutation(np.resize(levels, k // 32))).repeat(32)
    a = np.empty((k // 512, 16))
    for p in range(k // 512):
        a[p, :8] = np.random.permutation(np.resize(levels, 8))
        for g in range(8):
            far = levels[np.abs(levels - a[p, g]) >= 10]
            a[p, g + 8] = far[np.random.randint(len(far))]
    return np.exp2(a.ravel()).repeat(32)


BF16 = ml_dtypes.bfloat16


def bf(x):
    return np.asarray(x, np.float32).astype(BF16)


def f64(x):
    return np.asarray(x).astype(np.float64)


E2M1 = np.array([0.0, 0.5, 1.0, 1.5, 2.0, 3.0, 4.0, 6.0, -0.0, -0.5, -1.0, -1.5, -2.0, -3.0, -4.0, -6.0])


def pack_weight(w, fmt):
    k, n = w.shape
    w = f64(bf(w)).reshape(k // 32, 32, n)
    amax = np.abs(w).max(1)
    if fmt == "e4m3":
        byte = np.frexp(amax)[1] - 1 + 127 - 7
    else:
        mant, ex = np.frexp(amax / 6.0)
        byte = np.where(mant > 0.5, ex, ex - 1) + 127
    byte = np.clip(np.where(amax > 0, byte, 1), 1, 254)
    scaled = (w * np.exp2(127.0 - byte)[:, None, :]).reshape(k, n).astype(np.float32)
    by_word = np.ascontiguousarray(scaled.reshape(k // 512, 128, 4, n).transpose(0, 1, 3, 2))
    if fmt == "e4m3":
        words = by_word.astype(ml_dtypes.float8_e4m3fn).view(np.uint8)
    else:
        c = by_word.astype(ml_dtypes.float4_e2m1fn).view(np.uint8) & 0xF
        words = c[..., 0::2] | (c[..., 1::2] << 4)
    return np.ascontiguousarray(words), np.ascontiguousarray(byte.astype(np.uint8).reshape(k // 512, 16, n))


def unpack_weight(words, scales, fmt):
    g, p, n, _ = words.shape
    if fmt == "e4m3":
        vals = np.ascontiguousarray(words).view(ml_dtypes.float8_e4m3fn).astype(np.float64)
    else:
        nib = np.empty((g, p, n, 4), np.uint8)
        nib[..., 0::2] = words & 0xF
        nib[..., 1::2] = words >> 4
        vals = E2M1[nib]
    vals = vals * np.repeat(np.exp2(scales.astype(np.float64) - 127.0), 8, axis=1)[..., None]
    return vals.transpose(0, 1, 3, 2).reshape(g * 512, n)
def pack4(w):
    words, scales = pack_weight(w, "e2m1")
    return words.reshape(words.shape[0], 128, -1), scales


def unpack4(words, scales):
    return unpack_weight(words.reshape(words.shape[0], 128, -1, 2), scales, "e2m1")


def planes(Y):
    n, m = Y.shape
    b = f64(bf(Y)).reshape(n // 32, 32, m)
    amax = np.abs(b).max(1)
    byte = np.clip(np.where(amax > 0, np.frexp(amax)[1] - 1 + 127 - 7, 1), 1, 254)
    codes = (b * np.exp2(127.0 - byte)[:, None, :]).reshape(n, m).astype(np.float32).astype(ml_dtypes.float8_e4m3fn).view(np.uint8)
    words = codes.reshape(n // 512, 128, 4, m).transpose(0, 1, 3, 2)
    return np.ascontiguousarray(words), np.ascontiguousarray(byte.astype(np.uint8).reshape(n // 512, 16, m))


B, N, D, M = 4, 1024, 256, 512
M2 = 2 * M


def setup_inputs():
    s, t = mx_kscale(N), mx_kscale(M2)
    v = bf(np.random.standard_normal((B, N, D)) * s[None, :, None])
    enc = np.random.standard_normal((M2, N)) / np.sqrt(N) / s[None, :]
    enc_words, enc_scales = pack4(enc.T)
    dec = np.random.standard_normal((N, M2)) / np.sqrt(M2) / t[None, :]
    dec_words, dec_scales = pack4(dec.T)
    return {"v": v,
            "enc_words": enc_words,
            "enc_scales": enc_scales,
            "dec_words": dec_words,
            "dec_scales": dec_scales,
            "alpha": bf(0.5 + 0.5 * np.random.standard_normal((M, D))),
            "omega": bf(np.random.standard_normal(M)),
            "beta": bf(np.random.standard_normal((M2, D)) * t[:, None])}


def pole_response(alpha, omega):
    s = np.log1p(np.exp(alpha))
    w = omega[:, None]
    den = s * s + w * w
    return s / den, -w / den


def core(v, enc_words, enc_scales, dec_words, dec_scales, alpha, omega, beta):
    m = omega.shape[0]
    c = unpack4(enc_words, enc_scales).T @ mxq(f64(v), 1, "e4m3")
    cr = c[:, :m, :]
    ci = c[:, m:, :]
    hr, hi = pole_response(f64(alpha), f64(omega))
    yr = cr * hr - ci * hi
    yi = cr * hi + ci * hr
    z = np.concatenate([yr, yi], axis=1) * f64(beta)
    return unpack4(dec_words, dec_scales).T @ mxq(z, 1, "e4m3")


def reference(v, enc_words, enc_scales, dec_words, dec_scales, alpha, omega, beta):
    R_out = core(v, enc_words, enc_scales, dec_words, dec_scales, alpha, omega, beta)
    words, scales = planes(np.moveaxis(R_out, 1, 0).reshape(1024, -1))
    return R_out, words, scales

@@ -1,0 +1,310 @@
+from contextlib import ExitStack
+
+import concourse.mybir as mybir
+
+FLOPS = 2 * 2 * 1024 * 1024 * 1024
+
+F32 = mybir.dt.float32
+BF16 = mybir.dt.bfloat16
+I32 = mybir.dt.int32
+U32 = mybir.dt.uint32
+U8 = mybir.dt.uint8
+FP8X4 = mybir.dt.float8_e4m3fn_x4
+FP4X4 = mybir.dt.float4_e2m1fn_x4
+ACT = mybir.ActivationFunctionType
+ALU = mybir.AluOpType
+
+P = 128
+B = 4
+D = 256
+H = 128
+UNITS = [(0, 0), (1, 0), (0, 1), (1, 1), (2, 0), (2, 1), (3, 0), (3, 1)]
+
+
+def tile_laplacepoleresidueoperator_x2_kernel(
+    tc, v, enc_words, enc_scales, dec_words, dec_scales, alpha, omega, beta, out_0, out_1, out_2
+):
+    nc = tc.nc
+    with ExitStack() as ctx:
+        keep = ctx.enter_context(tc.tile_pool(name="keep", bufs=1))
+        work = ctx.enter_context(tc.tile_pool(name="work", bufs=2))
+        ps = ctx.enter_context(tc.psum_pool(name="ps", bufs=2))
+        ctx.enter_context(tc.manual_schedule())
+
+        def kt(name, shape, dt):
+            return keep.tile(shape, dt, name=name, align_bytes=64)
+
+        def wt(name, shape, dt, bufs=2):
+            return work.tile(shape, dt, name=name, align_bytes=64, bufs=bufs)
+
+        words_raw = [kt("enc_raw", [P, 2, 2048], U8), kt("dec_raw", [P, 2, 2048], U8)]
+        scale_raw = [kt("encs_raw", [P, 2, 1024], U8), kt("decs_raw", [P, 2, 1024], U8)]
+        words = [kt("enc_w", [P, 2, 2, 4, 256], U8), kt("dec_w", [P, 2, 2, 4, 256], U8)]
+        scales = [kt("enc_s", [P, 4, 4, 128], U8), kt("dec_s", [P, 4, 4, 128], U8)]
+        for i in range(2):
+            nc.gpsimd.memset(scale_raw[i][:].rearrange("p g n -> p (g n)").bitcast(I32), 0)
+
+        al = kt("al", [P, 4, D], BF16)
+        nc.sync.dma_start(out=al[:], in_=alpha.rearrange("(p t) d -> p t d", t=4))
+        om = kt("om", [P, 4], BF16)
+        nc.sync.dma_start(out=om[:], in_=omega.rearrange("(p t) -> p t", t=4))
+
+        def load_words(i, src):
+            nc.sync.dma_start(out=words_raw[i][:].bitcast(I32), in_=src.bitcast(I32).rearrange("g p n -> p g n"))
+
+        def load_scales(i, src):
+            for q in range(4):
+                nc.sync.dma_start(
+                    out=scale_raw[i][32 * q : 32 * q + 4, :, :].bitcast(I32),
+                    in_=src.bitcast(I32)[:, 4 * q : 4 * q + 4, :].rearrange("g q n -> q g n"),
+                )
+
+        vraw = [kt(f"vraw{b}", [P, 2, 4, D], BF16) for b in range(B)]
+
+        def load_v(b):
+            nc.sync.dma_start(
+                out=vraw[b][:].rearrange("p g t d -> p g (t d)"),
+                in_=v[b].rearrange("(g p t) d -> p g (t d)", g=2, t=4),
+            )
+
+        load_words(0, enc_words)
+        load_scales(0, enc_scales)
+        load_scales(1, dec_scales)
+        load_v(0)
+        load_v(1)
+        be = kt("be", [P, 2, 4, D], BF16)
+        nc.sync.dma_start(
+            out=be[:].rearrange("p g t d -> p g (t d)"), in_=beta.rearrange("(g p t) d -> p g (t d)", g=2, t=4)
+        )
+        load_words(1, dec_words)
+        load_v(2)
+        load_v(3)
+
+        def permute_words(i, x):
+            g, r = x // 2, x % 2
+            nc.vector.tensor_copy(
+                out=words[i][:, g, r].rearrange("p t (m e) -> p t m e", e=2),
+                in_=words_raw[i][:, g, r * 1024 : (r + 1) * 1024].rearrange("p (m t e) -> p t m e", t=4, e=2),
+            )
+
+        def permute_scales(i):
+            nc.vector.tensor_copy(
+                out=scales[i][:],
+                in_=scale_raw[i][:].rearrange("p g n -> p (g n)").rearrange("p (x m t) -> p x t m", x=4, t=4),
+            )
+
+        vi = [kt(f"vi{b}", [P, 2, D, 4], BF16) for b in range(B)]
+        vq = [kt(f"vq{b}", [P, 2, D], U32) for b in range(B)]
+        vs = [kt(f"vs{b}", [P, 2, D], U8) for b in range(B)]
+
+        def interleave_v(b, g, copy):
+            copy(
+                out=vi[b][:, g].rearrange("p (c i) t -> p c t i", i=4),
+                in_=vraw[b][:, g].rearrange("p t (c i) -> p c t i", i=4),
+            )
+
+        def quantize_v(b, g):
+            nc.vector.quantize_mx(
+                out=vq[b][:, g].bitcast(FP8X4),
+                scales=vs[b][:, g],
+                in_=vi[b][:, g].rearrange("p c t -> p (c t)"),
+            )
+
+        w32 = kt("w32", [P, 4], F32)
+        w2 = kt("w2", [P, 4], F32)
+        nc.gpsimd.tensor_copy(out=w32[:], in_=om[:])
+        nc.gpsimd.tensor_tensor(out=w2[:], in0=w32[:], in1=w32[:], op=ALU.mult)
+        w_b = w32[:].unsqueeze(1).to_broadcast([P, H, 4])
+        w2_b = w2[:].unsqueeze(1).to_broadcast([P, H, 4])
+
+        def half(name):
+            return [kt(f"{name}{h}", [P, H, 4], F32) for h in range(2)]
+
+        am = [kt(f"am{h}", [P, H, 4], BF16) for h in range(2)]
+        ex, sp, den, inv, hr, hw = half("ex"), half("sp"), half("den"), half("inv"), half("hr"), half("hw")
+        tA, tB, tC, tE = half("tA"), half("tB"), half("tC"), half("tE")
+
+        def cols(t3, h):
+            return t3[:, :, h * H : (h + 1) * H].rearrange("p t d -> p d t")
+
+        for h in range(2):
+            nc.vector.tensor_scalar_min(out=am[h][:], in0=cols(al, h), scalar1=40.0)
+        for h in range(2):
+            nc.scalar.activation(out=ex[h][:], in_=am[h][:], func=ACT.Exp)
+        for x in range(4):
+            permute_words(0, x)
+        for h in range(2):
+            nc.scalar.activation(out=ex[h][:], in_=ex[h][:], func=ACT.Ln, bias=1.0)
+        for h in range(2):
+            nc.vector.tensor_tensor(out=sp[h][:], in0=ex[h][:], in1=cols(al, h), op=ALU.max)
+            nc.scalar.activation(out=den[h][:], in_=sp[h][:], func=ACT.Square)
+        interleave_v(0, 0, nc.vector.tensor_copy)
+        interleave_v(1, 0, nc.scalar.copy)
+        for h in range(2):
+            nc.vector.tensor_tensor(out=den[h][:], in0=den[h][:], in1=w2_b, op=ALU.add)
+            nc.scalar.activation(out=den[h][:], in_=den[h][:], func=ACT.Ln)
+        permute_scales(0)
+        interleave_v(0, 1, nc.vector.tensor_copy)
+        for h in range(2):
+            nc.scalar.activation(out=inv[h][:], in_=den[h][:], func=ACT.Exp, scale=-1.0)
+        interleave_v(1, 1, nc.scalar.copy)
+        quantize_v(0, 0)
+        quantize_v(0, 1)
+        permute_words(1, 0)
+        permute_words(1, 1)
+
+        def tables(h):
+            br, bi = cols(be[:, 0], h), cols(be[:, 1], h)
+            nc.gpsimd.tensor_tensor(out=hw[h][:], in0=inv[h][:], in1=w_b, op=ALU.mult)
+            nc.vector.tensor_tensor(out=hr[h][:], in0=inv[h][:], in1=sp[h][:], op=ALU.mult)
+            nc.vector.tensor_tensor(out=tA[h][:], in0=br, in1=hr[h][:], op=ALU.mult)
+            nc.vector.tensor_tensor(out=tE[h][:], in0=bi, in1=hr[h][:], op=ALU.mult)
+            nc.gpsimd.tensor_tensor(out=tC[h][:], in0=bi, in1=hw[h][:], op=ALU.mult)
+            nc.vector.tensor_tensor(out=tB[h][:], in0=br, in1=hw[h][:], op=ALU.mult)
+
+        cr, ci, xt, zt, zq, zs, ob = {}, {}, {}, {}, {}, {}, {}
+        of = [kt(f"of{b}", [P, 2, 4, D], F32) for b in range(B)]
+        oq = [kt(f"oq{b}", [P, 2, D], U32) for b in range(B)]
+        osc = kt("osc", [P, 2, 1024], U8)
+
+        def weight(i, g, r, t):
+            return (
+                words[i][:, g, r, t].bitcast(FP4X4),
+                scales[i][:, 2 * g + r, t],
+            )
+
+        def product(i, bank, r, rhs, rhs_scale):
+            for t in range(4):
+                for g in range(2):
+                    lhs, lhs_scale = weight(i, g, r, t)
+                    nc.tensor.matmul_mx(
+                        out=bank[:, t, :],
+                        lhsT=lhs,
+                        lhsT_scale=lhs_scale,
+                        rhs=rhs(g),
+                        rhs_scale=rhs_scale(g),
+                        start=(g == 0),
+                        stop=(g == 1),
+                    )
+
+        def stage1(u):
+            b, h = UNITS[u]
+            sl = slice(h * H, (h + 1) * H)
+            cr[u] = ps.tile([P, 4, H], F32, name="cr")
+            ci[u] = ps.tile([P, 4, H], F32, name="ci")
+            for r, bank in ((0, cr[u]), (1, ci[u])):
+                product(0, bank, r, lambda g: vq[b][:, g, sl].bitcast(FP8X4), lambda g: vs[b][:, g, sl])
+
+        def mult(u, j):
+            h = UNITS[u][1]
+            bank = (cr, ci, cr, ci)[j][u]
+            table = (tA, tB, tC, tE)[j][h]
+            x = wt(f"x{j}", [P, H, 4], F32)
+            nc.vector.tensor_tensor(out=x[:], in0=bank[:].rearrange("p t c -> p c t"), in1=table[:], op=ALU.mult)
+            xt[u, j] = x
+
+        def add(u, r):
+            if r == 0:
+                zt[u] = wt("zt", [P, 2, H, 4], BF16)
+                nc.gpsimd.tensor_tensor(out=zt[u][:, 0], in0=xt[u, 0][:], in1=xt[u, 1][:], op=ALU.add)
+            else:
+                nc.gpsimd.tensor_tensor(out=zt[u][:, 1], in0=xt[u, 3][:], in1=xt[u, 2][:], op=ALU.subtract)
+
+        def quantize_z(u):
+            zq[u] = wt("zq", [P, 2, H], U32)
+            zs[u] = wt("zs", [P, 2, H], U8)
+            nc.vector.quantize_mx(
+                out=zq[u][:].rearrange("p g c -> p (g c)").bitcast(FP8X4),
+                scales=zs[u][:].rearrange("p g c -> p (g c)"),
+                in_=zt[u][:].rearrange("p g c t -> p (g c t)"),
+            )
+
+        def stage2(u):
+            b, h = UNITS[u]
+            sl = slice(h * H, (h + 1) * H)
+            ob[u] = wt("ob", [P, 2, H, 4], BF16, bufs=3)
+            for r in range(2):
+                bank = ps.tile([P, 4, H], F32, name=f"o{r}")
+                product(1, bank, r, lambda g: zq[u][:, g].bitcast(FP8X4), lambda g: zs[u][:, g])
+                nc.scalar.copy(out=of[b][:, r, :, sl], in_=bank[:])
+                nc.scalar.copy(out=ob[u][:, r], in_=bank[:].rearrange("p t c -> p c t"))
+
+        def quantize_out(u):
+            b, h = UNITS[u]
+            for r in range(2):
+                nc.vector.quantize_mx(
+                    out=oq[b][:, r, h * H : (h + 1) * H].bitcast(FP8X4),
+                    scales=osc[:, r, b * D + h * H : b * D + (h + 1) * H],
+                    in_=ob[u][:, r].rearrange("p c t -> p (c t)"),
+                )
+
+        out_words = out_1.rearrange("g p m t -> g p (m t)").bitcast(I32).rearrange("g p m -> p g m")
+        out_scales = out_2.bitcast(I32)
+
+        def store(u):
+            b, h = UNITS[u]
+            if b < 3:
+                if h == 1:
+                    nc.sync.dma_start(
+                        out=out_0[b].rearrange("(g p t) d -> p g (t d)", g=2, t=4),
+                        in_=of[b][:].rearrange("p g t d -> p g (t d)"),
+                    )
+            else:
+                sl = slice(h * H, (h + 1) * H)
+                for g in range(2):
+                    nc.sync.dma_start(
+                        out=out_0[b, 512 * g : 512 * (g + 1), sl].rearrange("(p t) d -> p t d", t=4),
+                        in_=of[b][:, g, :, sl],
+                    )
+
+        def store_planes(u):
+            b, h = UNITS[u]
+            if h == 1:
+                nc.sync.dma_start(out=out_words[:, :, b * D : (b + 1) * D], in_=oq[b][:].bitcast(I32))
+            if (b, h) == (2, 1) or (b, h) == (3, 1):
+                lo, hi = (0, 192) if b == 2 else (192, 256)
+                for q in range(4):
+                    nc.sync.dma_start(
+                        out=out_scales[:, 4 * q : 4 * q + 4, lo:hi].rearrange("g q n -> q g n"),
+                        in_=osc[32 * q : 32 * q + 4, :, :].bitcast(I32)[:, :, lo:hi],
+                    )
+
+        n = len(UNITS)
+        stage1(0)
+        tables(0)
+        quantize_v(1, 0)
+        quantize_v(1, 1)
+
+        for k in range(n + 3):
+            if k + 1 < n:
+                stage1(k + 1)
+            if k < n:
+                mult(k, 0)
+            if k >= 3:
+                quantize_out(k - 3)
+                store_planes(k - 3)
+            if k < n:
+                mult(k, 1)
+                add(k, 0)
+            if 1 <= k <= n:
+                quantize_z(k - 1)
+                stage2(k - 1)
+                store(k - 1)
+            if k < n:
+                mult(k, 2)
+                mult(k, 3)
+                add(k, 1)
+            if k == 0:
+                permute_words(1, 2)
+                permute_words(1, 3)
+                permute_scales(1)
+                tables(1)
+                for g in range(2):
+                    interleave_v(2, g, nc.scalar.copy)
+            if k == 1:
+                for g in range(2):
+                    quantize_v(2, g)
+                    interleave_v(3, g, nc.scalar.copy)
+            if k == 3:
+                for g in range(2):
+                    quantize_v(3, g)

@@ -18,7 +18,7 @@ P = 128
 B = 4
 D = 256
 H = 128
-UNITS = [(0, 0), (1, 0), (0, 1), (1, 1), (2, 0), (2, 1), (3, 0), (3, 1)]
+UNITS = [(b, h) for b in range(B) for h in range(2)]
 
 
 def tile_laplacepoleresidueoperator_x2_kernel(
@@ -71,11 +71,11 @@ def tile_laplacepoleresidueoperator_x2_kernel(
         load_scales(0, enc_scales)
         load_scales(1, dec_scales)
         load_v(0)
-        load_v(1)
         be = kt("be", [P, 2, 4, D], BF16)
         nc.sync.dma_start(
             out=be[:].rearrange("p g t d -> p g (t d)"), in_=beta.rearrange("(g p t) d -> p g (t d)", g=2, t=4)
         )
+        load_v(1)
         load_words(1, dec_words)
         load_v(2)
         load_v(3)
@@ -112,57 +112,40 @@ def tile_laplacepoleresidueoperator_x2_kernel(
 
         w32 = kt("w32", [P, 4], F32)
         w2 = kt("w2", [P, 4], F32)
+        wn = kt("wn", [P, 4], F32)
         nc.gpsimd.tensor_copy(out=w32[:], in_=om[:])
         nc.gpsimd.tensor_tensor(out=w2[:], in0=w32[:], in1=w32[:], op=ALU.mult)
-        w_b = w32[:].unsqueeze(1).to_broadcast([P, H, 4])
-        w2_b = w2[:].unsqueeze(1).to_broadcast([P, H, 4])
+        nc.gpsimd.tensor_scalar(out=wn[:], in0=w32[:], scalar1=-1.0, scalar2=0.0, op0=ALU.mult, op1=ALU.add)
+        am = kt("am", [P, 4, D], BF16)
+        ex, sp, den, inv = [kt(x, [P, 4, D], F32) for x in ("ex", "sp", "den", "inv")]
+        gain = [kt(f"gain{r}", [P, 4, D], F32) for r in range(2)]
+        HALF = (slice(0, 2), slice(2, 4))
 
-        def half(name):
-            return [kt(f"{name}{h}", [P, H, 4], F32) for h in range(2)]
-
-        am = [kt(f"am{h}", [P, H, 4], BF16) for h in range(2)]
-        ex, sp, den, inv, hr, hw = half("ex"), half("sp"), half("den"), half("inv"), half("hr"), half("hw")
-        tA, tB, tC, tE = half("tA"), half("tB"), half("tC"), half("tE")
-
-        def cols(t3, h):
-            return t3[:, :, h * H : (h + 1) * H].rearrange("p t d -> p d t")
-
-        for h in range(2):
-            nc.vector.tensor_scalar_min(out=am[h][:], in0=cols(al, h), scalar1=40.0)
-        for h in range(2):
-            nc.scalar.activation(out=ex[h][:], in_=am[h][:], func=ACT.Exp)
+        nc.vector.tensor_scalar_min(out=am[:], in0=al[:], scalar1=40.0)
+        nc.scalar.activation(out=ex[:], in_=am[:], func=ACT.Exp)
         for x in range(4):
             permute_words(0, x)
-        for h in range(2):
-            nc.scalar.activation(out=ex[h][:], in_=ex[h][:], func=ACT.Ln, bias=1.0)
-        for h in range(2):
-            nc.vector.tensor_tensor(out=sp[h][:], in0=ex[h][:], in1=cols(al, h), op=ALU.max)
-            nc.scalar.activation(out=den[h][:], in_=sp[h][:], func=ACT.Square)
-        interleave_v(0, 0, nc.vector.tensor_copy)
-        interleave_v(1, 0, nc.scalar.copy)
-        for h in range(2):
-            nc.vector.tensor_tensor(out=den[h][:], in0=den[h][:], in1=w2_b, op=ALU.add)
-            nc.scalar.activation(out=den[h][:], in_=den[h][:], func=ACT.Ln)
+        for s in HALF:
+            nc.scalar.activation(out=ex[:, s], in_=ex[:, s], func=ACT.Ln, bias=1.0)
+        for s in HALF:
+            nc.vector.tensor_tensor(out=sp[:, s], in0=ex[:, s], in1=al[:, s], op=ALU.max)
+        for g in range(2):
+            interleave_v(0, g, nc.scalar.copy)
         permute_scales(0)
-        interleave_v(0, 1, nc.vector.tensor_copy)
-        for h in range(2):
-            nc.scalar.activation(out=inv[h][:], in_=den[h][:], func=ACT.Exp, scale=-1.0)
-        interleave_v(1, 1, nc.scalar.copy)
-        quantize_v(0, 0)
-        quantize_v(0, 1)
+        for s in HALF:
+            nc.scalar.activation(out=den[:, s], in_=sp[:, s], func=ACT.Square)
+        for t in range(4):
+            nc.scalar.activation(out=den[:, t], in_=den[:, t], func=ACT.Ln, bias=w2[:, t : t + 1])
+        for s in HALF:
+            nc.scalar.activation(out=inv[:, s], in_=den[:, s], func=ACT.Exp, scale=-1.0)
+        for g in range(2):
+            quantize_v(0, g)
         permute_words(1, 0)
         permute_words(1, 1)
+        for g in range(2):
+            interleave_v(1, g, nc.scalar.copy)
 
-        def tables(h):
-            br, bi = cols(be[:, 0], h), cols(be[:, 1], h)
-            nc.gpsimd.tensor_tensor(out=hw[h][:], in0=inv[h][:], in1=w_b, op=ALU.mult)
-            nc.vector.tensor_tensor(out=hr[h][:], in0=inv[h][:], in1=sp[h][:], op=ALU.mult)
-            nc.vector.tensor_tensor(out=tA[h][:], in0=br, in1=hr[h][:], op=ALU.mult)
-            nc.vector.tensor_tensor(out=tE[h][:], in0=bi, in1=hr[h][:], op=ALU.mult)
-            nc.gpsimd.tensor_tensor(out=tC[h][:], in0=bi, in1=hw[h][:], op=ALU.mult)
-            nc.vector.tensor_tensor(out=tB[h][:], in0=br, in1=hw[h][:], op=ALU.mult)
-
-        cr, ci, xt, zt, zq, zs, ob = {}, {}, {}, {}, {}, {}, {}
+        cr, ci, st, zt, zq, zs, ob = {}, {}, {}, {}, {}, {}, {}
         of = [kt(f"of{b}", [P, 2, 4, D], F32) for b in range(B)]
         oq = [kt(f"oq{b}", [P, 2, D], U32) for b in range(B)]
         osc = kt("osc", [P, 2, 1024], U8)
@@ -195,20 +178,36 @@ def tile_laplacepoleresidueoperator_x2_kernel(
             for r, bank in ((0, cr[u]), (1, ci[u])):
                 product(0, bank, r, lambda g: vq[b][:, g, sl].bitcast(FP8X4), lambda g: vs[b][:, g, sl])
 
-        def mult(u, j):
+        def combine(u):
             h = UNITS[u][1]
-            bank = (cr, ci, cr, ci)[j][u]
-            table = (tA, tB, tC, tE)[j][h]
-            x = wt(f"x{j}", [P, H, 4], F32)
-            nc.vector.tensor_tensor(out=x[:], in0=bank[:].rearrange("p t c -> p c t"), in1=table[:], op=ALU.mult)
-            xt[u, j] = x
+            sl = slice(h * H, (h + 1) * H)
+            st[u, 0] = wt("s0", [P, 4, H], F32)
+            st[u, 1] = wt("s1", [P, 4, H], F32)
+            for r, bank in ((0, cr[u]), (1, ci[u])):
+                nc.vector.tensor_tensor(out=st[u, r][:], in0=bank[:], in1=sp[:, :, sl], op=ALU.mult)
+            for r, bank, coeff in ((0, ci[u], w32), (1, cr[u], wn)):
+                s = st[u, r]
+                for t in range(4):
+                    nc.vector.scalar_tensor_tensor(
+                        out=s[:, t],
+                        in0=bank[:, t],
+                        scalar=coeff[:, t : t + 1],
+                        in1=s[:, t],
+                        op0=ALU.mult,
+                        op1=ALU.add,
+                    )
 
-        def add(u, r):
+        def gain_z(u, r, engine):
+            h = UNITS[u][1]
+            sl = slice(h * H, (h + 1) * H)
             if r == 0:
-                zt[u] = wt("zt", [P, 2, H, 4], BF16)
-                nc.gpsimd.tensor_tensor(out=zt[u][:, 0], in0=xt[u, 0][:], in1=xt[u, 1][:], op=ALU.add)
-            else:
-                nc.gpsimd.tensor_tensor(out=zt[u][:, 1], in0=xt[u, 3][:], in1=xt[u, 2][:], op=ALU.subtract)
+                zt[u] = wt("zt", [P, 2, H, 4], BF16, bufs=1)
+            engine.tensor_tensor(
+                out=zt[u][:, r].rearrange("p (c i) t -> p c t i", i=4),
+                in0=st[u, r][:].rearrange("p t (c i) -> p c t i", i=4),
+                in1=gain[r][:, :, sl].rearrange("p t (c i) -> p c t i", i=4),
+                op=ALU.mult,
+            )
 
         def quantize_z(u):
             zq[u] = wt("zq", [P, 2, H], U32)
@@ -219,6 +218,24 @@ def tile_laplacepoleresidueoperator_x2_kernel(
                 in_=zt[u][:].rearrange("p g c t -> p (g c t)"),
             )
 
+        def quantize_out_half(u, r):
+            b, h = UNITS[u]
+            nc.vector.quantize_mx(
+                out=oq[b][:, r, h * H : (h + 1) * H].bitcast(FP8X4),
+                scales=osc[:, r, b * D + h * H : b * D + (h + 1) * H],
+                in_=ob[u][:, r].rearrange("p c t -> p (c t)"),
+            )
+
+        def finish(u):
+            b, h = UNITS[u]
+            sl = slice(h * H, (h + 1) * H)
+            for r in range(2):
+                nc.vector.tensor_copy(
+                    out=ob[u][:, r].rearrange("p (c i) t -> p c t i", i=4),
+                    in_=of[b][:, r, :, sl].rearrange("p t (c i) -> p c t i", i=4),
+                )
+                quantize_out_half(u, r)
+
         def stage2(u):
             b, h = UNITS[u]
             sl = slice(h * H, (h + 1) * H)
@@ -227,16 +244,8 @@ def tile_laplacepoleresidueoperator_x2_kernel(
                 bank = ps.tile([P, 4, H], F32, name=f"o{r}")
                 product(1, bank, r, lambda g: zq[u][:, g].bitcast(FP8X4), lambda g: zs[u][:, g])
                 nc.scalar.copy(out=of[b][:, r, :, sl], in_=bank[:])
-                nc.scalar.copy(out=ob[u][:, r], in_=bank[:].rearrange("p t c -> p c t"))
-
-        def quantize_out(u):
-            b, h = UNITS[u]
-            for r in range(2):
-                nc.vector.quantize_mx(
-                    out=oq[b][:, r, h * H : (h + 1) * H].bitcast(FP8X4),
-                    scales=osc[:, r, b * D + h * H : b * D + (h + 1) * H],
-                    in_=ob[u][:, r].rearrange("p c t -> p (c t)"),
-                )
+                if u < len(UNITS) - 2:
+                    nc.scalar.copy(out=ob[u][:, r], in_=bank[:].rearrange("p t c -> p c t"))
 
         out_words = out_1.rearrange("g p m t -> g p (m t)").bitcast(I32).rearrange("g p m -> p g m")
         out_scales = out_2.bitcast(I32)
@@ -271,40 +280,39 @@ def tile_laplacepoleresidueoperator_x2_kernel(
 
         n = len(UNITS)
         stage1(0)
-        tables(0)
-        quantize_v(1, 0)
-        quantize_v(1, 1)
-
-        for k in range(n + 3):
+        for k in range(n + 1):
             if k + 1 < n:
                 stage1(k + 1)
             if k < n:
-                mult(k, 0)
-            if k >= 3:
-                quantize_out(k - 3)
-                store_planes(k - 3)
-            if k < n:
-                mult(k, 1)
-                add(k, 0)
-            if 1 <= k <= n:
-                quantize_z(k - 1)
-                stage2(k - 1)
-                store(k - 1)
-            if k < n:
-                mult(k, 2)
-                mult(k, 3)
-                add(k, 1)
+                combine(k)
             if k == 0:
                 permute_words(1, 2)
                 permute_words(1, 3)
                 permute_scales(1)
-                tables(1)
                 for g in range(2):
-                    interleave_v(2, g, nc.scalar.copy)
-            if k == 1:
+                    quantize_v(1, g)
+                for r in (1, 0):
+                    for s in HALF:
+                        nc.vector.tensor_tensor(out=gain[r][:, s], in0=be[:, r, s], in1=inv[:, s], op=ALU.mult)
+                for b in (2, 3):
+                    for g in range(2):
+                        interleave_v(b, g, nc.scalar.copy)
+            if k in (2, 4):
                 for g in range(2):
-                    quantize_v(2, g)
-                    interleave_v(3, g, nc.scalar.copy)
-            if k == 3:
-                for g in range(2):
-                    quantize_v(3, g)
+                    quantize_v(k // 2 + 1, g)
+            if k >= 3:
+                for r in range(2):
+                    quantize_out_half(k - 3, r)
+                store_planes(k - 3)
+            if k >= 2:
+                store(k - 2)
+            if k >= 1:
+                for r in range(2):
+                    gain_z(k - 1, r, nc.vector if k == n else nc.gpsimd)
+                quantize_z(k - 1)
+                stage2(k - 1)
+        finish(n - 2)
+        store_planes(n - 2)
+        store(n - 1)
+        finish(n - 1)
+        store_planes(n - 1)

@@ -38,24 +38,20 @@ def tile_laplacepoleresidueoperator_x2_kernel(
             return work.tile(shape, dt, name=name, align_bytes=64, bufs=bufs)
 
         words_raw = [kt("enc_raw", [P, 2, 2048], U8), kt("dec_raw", [P, 2, 2048], U8)]
-        scale_raw = [kt("encs_raw", [P, 2, 1024], U8), kt("decs_raw", [P, 2, 1024], U8)]
+        scale_raw = kt("encs_raw", [P, 2, 1024], U8)
         words = [kt("enc_w", [P, 2, 2, 4, 256], U8), kt("dec_w", [P, 2, 2, 4, 256], U8)]
-        scales = [kt("enc_s", [P, 4, 4, 128], U8), kt("dec_s", [P, 4, 4, 128], U8)]
-        for i in range(2):
-            nc.gpsimd.memset(scale_raw[i][:].rearrange("p g n -> p (g n)").bitcast(I32), 0)
+        scales = [kt("sc_enc", [P, 4, 4, 128], U8), kt("decs_p", [P, 4, 4, 128], U8)]
+        nc.gpsimd.memset(scale_raw[:].rearrange("p g n -> p (g n)").bitcast(I32), 0)
+        nc.gpsimd.memset(scales[1][:].rearrange("p x t m -> p (x t m)").bitcast(I32), 0)
 
-        al = kt("al", [P, 4, D], BF16)
-        nc.sync.dma_start(out=al[:], in_=alpha.rearrange("(p t) d -> p t d", t=4))
-        om = kt("om", [P, 4], BF16)
-        nc.sync.dma_start(out=om[:], in_=omega.rearrange("(p t) -> p t", t=4))
-
-        def load_words(i, src):
-            nc.sync.dma_start(out=words_raw[i][:].bitcast(I32), in_=src.bitcast(I32).rearrange("g p n -> p g n"))
+        def load_words(i, src, g):
+            nc.sync.dma_start(out=words_raw[i][:, g].bitcast(I32), in_=src.bitcast(I32)[g])
 
         def load_scales(i, src):
             for q in range(4):
+                lo = 32 * q + 4 * i
                 nc.sync.dma_start(
-                    out=scale_raw[i][32 * q : 32 * q + 4, :, :].bitcast(I32),
+                    out=scale_raw[lo : lo + 4, :, :].bitcast(I32),
                     in_=src.bitcast(I32)[:, 4 * q : 4 * q + 4, :].rearrange("g q n -> q g n"),
                 )
 
@@ -67,16 +63,22 @@ def tile_laplacepoleresidueoperator_x2_kernel(
                 in_=v[b].rearrange("(g p t) d -> p g (t d)", g=2, t=4),
             )
 
-        load_words(0, enc_words)
+        load_words(0, enc_words, 0)
+        load_words(0, enc_words, 1)
+        al = kt("al", [P, 4, D], BF16)
+        nc.sync.dma_start(out=al[:], in_=alpha.rearrange("(p t) d -> p t d", t=4))
+        om = kt("om", [P, 4], BF16)
+        nc.sync.dma_start(out=om[:], in_=omega.rearrange("(p t) -> p t", t=4))
         load_scales(0, enc_scales)
         load_scales(1, dec_scales)
         load_v(0)
+        load_words(1, dec_words, 0)
+        load_words(1, dec_words, 1)
+        load_v(1)
         be = kt("be", [P, 2, 4, D], BF16)
         nc.sync.dma_start(
             out=be[:].rearrange("p g t d -> p g (t d)"), in_=beta.rearrange("(g p t) d -> p g (t d)", g=2, t=4)
         )
-        load_v(1)
-        load_words(1, dec_words)
         load_v(2)
         load_v(3)
 
@@ -87,13 +89,22 @@ def tile_laplacepoleresidueoperator_x2_kernel(
                 in_=words_raw[i][:, g, r * 1024 : (r + 1) * 1024].rearrange("p (m t e) -> p t m e", t=4, e=2),
             )
 
-        def permute_scales(i):
+        def permute_scales():
             nc.vector.tensor_copy(
-                out=scales[i][:],
-                in_=scale_raw[i][:].rearrange("p g n -> p (g n)").rearrange("p (x m t) -> p x t m", x=4, t=4),
+                out=scales[0][:],
+                in_=scale_raw[:].rearrange("p g n -> p (g n)").rearrange("p (x m t) -> p x t m", x=4, t=4),
             )
+            for q in range(4):
+                lo = 32 * q
+                nc.sync.dma_start(
+                    out=scales[1][lo : lo + 4].rearrange("p x t m -> p (x t m)").bitcast(I32),
+                    in_=scales[0][lo + 4 : lo + 8].rearrange("p x t m -> p (x t m)").bitcast(I32),
+                )
 
-        vi = [kt(f"vi{b}", [P, 2, D, 4], BF16) for b in range(B)]
+        def vi_tile(b):
+            return keep.tile([P, 2, D, 4], BF16, name=f"vi{max(b, 1)}", align_bytes=64)
+
+        vi = {b: vi_tile(b) for b in (0, 2, 3)}
         vq = [kt(f"vq{b}", [P, 2, D], U32) for b in range(B)]
         vs = [kt(f"vs{b}", [P, 2, D], U8) for b in range(B)]
 
@@ -103,11 +114,14 @@ def tile_laplacepoleresidueoperator_x2_kernel(
                 in_=vraw[b][:, g].rearrange("p t (c i) -> p c t i", i=4),
             )
 
-        def quantize_v(b, g):
+        def gpsimd_copy(out, in_):
+            nc.gpsimd.tensor_scalar(out=out, in0=in_, scalar1=1.0, scalar2=0.0, op0=ALU.mult, op1=ALU.add)
+
+        def quantize_v(b):
             nc.vector.quantize_mx(
-                out=vq[b][:, g].bitcast(FP8X4),
-                scales=vs[b][:, g],
-                in_=vi[b][:, g].rearrange("p c t -> p (c t)"),
+                out=vq[b][:].rearrange("p g c -> p (g c)").bitcast(FP8X4),
+                scales=vs[b][:].rearrange("p g c -> p (g c)"),
+                in_=vi[b][:].rearrange("p g c t -> p (g c t)"),
             )
 
         w32 = kt("w32", [P, 4], F32)
@@ -121,29 +135,33 @@ def tile_laplacepoleresidueoperator_x2_kernel(
         gain = [kt(f"gain{r}", [P, 4, D], F32) for r in range(2)]
         HALF = (slice(0, 2), slice(2, 4))
 
+        permute_words(0, 0)
+        permute_words(0, 1)
         nc.vector.tensor_scalar_min(out=am[:], in0=al[:], scalar1=40.0)
         nc.scalar.activation(out=ex[:], in_=am[:], func=ACT.Exp)
-        for x in range(4):
-            permute_words(0, x)
+        permute_words(0, 2)
+        permute_words(0, 3)
+        permute_scales()
+        permute_words(1, 0)
+        permute_words(1, 1)
         for s in HALF:
             nc.scalar.activation(out=ex[:, s], in_=ex[:, s], func=ACT.Ln, bias=1.0)
         for s in HALF:
             nc.vector.tensor_tensor(out=sp[:, s], in0=ex[:, s], in1=al[:, s], op=ALU.max)
         for g in range(2):
             interleave_v(0, g, nc.scalar.copy)
-        permute_scales(0)
         for s in HALF:
             nc.scalar.activation(out=den[:, s], in_=sp[:, s], func=ACT.Square)
         for t in range(4):
             nc.scalar.activation(out=den[:, t], in_=den[:, t], func=ACT.Ln, bias=w2[:, t : t + 1])
         for s in HALF:
             nc.scalar.activation(out=inv[:, s], in_=den[:, s], func=ACT.Exp, scale=-1.0)
+        permute_words(1, 2)
+        quantize_v(0)
+        permute_words(1, 3)
+        vi[1] = vi_tile(1)
         for g in range(2):
-            quantize_v(0, g)
-        permute_words(1, 0)
-        permute_words(1, 1)
-        for g in range(2):
-            interleave_v(1, g, nc.scalar.copy)
+            interleave_v(1, g, gpsimd_copy)
 
         cr, ci, st, zt, zq, zs, ob = {}, {}, {}, {}, {}, {}, {}
         of = [kt(f"of{b}", [P, 2, 4, D], F32) for b in range(B)]
@@ -252,7 +270,7 @@ def tile_laplacepoleresidueoperator_x2_kernel(
 
         def store(u):
             b, h = UNITS[u]
-            if b < 3:
+            if b < 2:
                 if h == 1:
                     nc.sync.dma_start(
                         out=out_0[b].rearrange("(g p t) d -> p g (t d)", g=2, t=4),
@@ -286,11 +304,7 @@ def tile_laplacepoleresidueoperator_x2_kernel(
             if k < n:
                 combine(k)
             if k == 0:
-                permute_words(1, 2)
-                permute_words(1, 3)
-                permute_scales(1)
-                for g in range(2):
-                    quantize_v(1, g)
+                quantize_v(1)
                 for r in (1, 0):
                     for s in HALF:
                         nc.vector.tensor_tensor(out=gain[r][:, s], in0=be[:, r, s], in1=inv[:, s], op=ALU.mult)
@@ -298,8 +312,7 @@ def tile_laplacepoleresidueoperator_x2_kernel(
                     for g in range(2):
                         interleave_v(b, g, nc.scalar.copy)
             if k in (2, 4):
-                for g in range(2):
-                    quantize_v(k // 2 + 1, g)
+                quantize_v(k // 2 + 1)
             if k >= 3:
                 for r in range(2):
                     quantize_out_half(k - 3, r)

from contextlib import ExitStack

import concourse.mybir as mybir

FLOPS = 2 * 2 * 1024 * 1024 * 1024

F32 = mybir.dt.float32
BF16 = mybir.dt.bfloat16
I32 = mybir.dt.int32
U32 = mybir.dt.uint32
U8 = mybir.dt.uint8
FP8X4 = mybir.dt.float8_e4m3fn_x4
FP4X4 = mybir.dt.float4_e2m1fn_x4
ACT = mybir.ActivationFunctionType
ALU = mybir.AluOpType

P = 128
B = 4
D = 256
H = 128
UNITS = [(b, h) for b in range(B) for h in range(2)]


def tile_laplacepoleresidueoperator_x2_kernel(
    tc, v, enc_words, enc_scales, dec_words, dec_scales, alpha, omega, beta, out_0, out_1, out_2
):
    nc = tc.nc
    with ExitStack() as ctx:
        keep = ctx.enter_context(tc.tile_pool(name="keep", bufs=1))
        work = ctx.enter_context(tc.tile_pool(name="work", bufs=2))
        ps = ctx.enter_context(tc.psum_pool(name="ps", bufs=2))
        ctx.enter_context(tc.manual_schedule())

        def kt(name, shape, dt):
            return keep.tile(shape, dt, name=name, align_bytes=64)

        def wt(name, shape, dt, bufs=2):
            return work.tile(shape, dt, name=name, align_bytes=64, bufs=bufs)

        words_raw = [kt("enc_raw", [P, 2, 2048], U8), kt("dec_raw", [P, 2, 2048], U8)]
        scale_raw = kt("encs_raw", [P, 2, 1024], U8)
        words = [kt("enc_w", [P, 2, 2, 4, 256], U8), kt("dec_w", [P, 2, 2, 4, 256], U8)]
        scales = [kt("sc_enc", [P, 4, 4, 128], U8), kt("decs_p", [P, 4, 4, 128], U8)]
        nc.gpsimd.memset(scale_raw[:].rearrange("p g n -> p (g n)").bitcast(I32), 0)
        nc.gpsimd.memset(scales[1][:].rearrange("p x t m -> p (x t m)").bitcast(I32), 0)

        def load_words(i, src, g):
            nc.sync.dma_start(out=words_raw[i][:, g].bitcast(I32), in_=src.bitcast(I32)[g])

        def load_scales(i, src):
            for q in range(4):
                lo = 32 * q + 4 * i
                nc.sync.dma_start(
                    out=scale_raw[lo : lo + 4, :, :].bitcast(I32),
                    in_=src.bitcast(I32)[:, 4 * q : 4 * q + 4, :].rearrange("g q n -> q g n"),
                )

        vraw = [kt(f"vraw{b}", [P, 2, 4, D], BF16) for b in range(B)]

        def load_v(b):
            nc.sync.dma_start(
                out=vraw[b][:].rearrange("p g t d -> p g (t d)"),
                in_=v[b].rearrange("(g p t) d -> p g (t d)", g=2, t=4),
            )

        load_words(0, enc_words, 0)
        load_words(0, enc_words, 1)
        al = kt("al", [P, 4, D], BF16)
        nc.sync.dma_start(out=al[:], in_=alpha.rearrange("(p t) d -> p t d", t=4))
        om = kt("om", [P, 4], BF16)
        nc.sync.dma_start(out=om[:], in_=omega.rearrange("(p t) -> p t", t=4))
        load_scales(0, enc_scales)
        load_scales(1, dec_scales)
        load_v(0)
        load_words(1, dec_words, 0)
        load_words(1, dec_words, 1)
        load_v(1)
        be = kt("be", [P, 2, 4, D], BF16)
        nc.sync.dma_start(
            out=be[:].rearrange("p g t d -> p g (t d)"), in_=beta.rearrange("(g p t) d -> p g (t d)", g=2, t=4)
        )
        load_v(2)
        load_v(3)

        def permute_words(i, x):
            g, r = x // 2, x % 2
            nc.vector.tensor_copy(
                out=words[i][:, g, r].rearrange("p t (m e) -> p t m e", e=2),
                in_=words_raw[i][:, g, r * 1024 : (r + 1) * 1024].rearrange("p (m t e) -> p t m e", t=4, e=2),
            )

        def permute_scales():
            nc.vector.tensor_copy(
                out=scales[0][:],
                in_=scale_raw[:].rearrange("p g n -> p (g n)").rearrange("p (x m t) -> p x t m", x=4, t=4),
            )
            for q in range(4):
                lo = 32 * q
                nc.sync.dma_start(
                    out=scales[1][lo : lo + 4].rearrange("p x t m -> p (x t m)").bitcast(I32),
                    in_=scales[0][lo + 4 : lo + 8].rearrange("p x t m -> p (x t m)").bitcast(I32),
                )

        def vi_tile(b):
            return keep.tile([P, 2, D, 4], BF16, name=f"vi{max(b, 1)}", align_bytes=64)

        vi = {b: vi_tile(b) for b in (0, 2, 3)}
        vq = [kt(f"vq{b}", [P, 2, D], U32) for b in range(B)]
        vs = [kt(f"vs{b}", [P, 2, D], U8) for b in range(B)]

        def interleave_v(b, g, copy):
            copy(
                out=vi[b][:, g].rearrange("p (c i) t -> p c t i", i=4),
                in_=vraw[b][:, g].rearrange("p t (c i) -> p c t i", i=4),
            )

        def gpsimd_copy(out, in_):
            nc.gpsimd.tensor_scalar(out=out, in0=in_, scalar1=1.0, scalar2=0.0, op0=ALU.mult, op1=ALU.add)

        def quantize_v(b):
            nc.vector.quantize_mx(
                out=vq[b][:].rearrange("p g c -> p (g c)").bitcast(FP8X4),
                scales=vs[b][:].rearrange("p g c -> p (g c)"),
                in_=vi[b][:].rearrange("p g c t -> p (g c t)"),
            )

        w32 = kt("w32", [P, 4], F32)
        w2 = kt("w2", [P, 4], F32)
        wn = kt("wn", [P, 4], F32)
        nc.gpsimd.tensor_copy(out=w32[:], in_=om[:])
        nc.gpsimd.tensor_tensor(out=w2[:], in0=w32[:], in1=w32[:], op=ALU.mult)
        nc.gpsimd.tensor_scalar(out=wn[:], in0=w32[:], scalar1=-1.0, scalar2=0.0, op0=ALU.mult, op1=ALU.add)
        am = kt("am", [P, 4, D], BF16)
        ex, sp, den, inv = [kt(x, [P, 4, D], F32) for x in ("ex", "sp", "den", "inv")]
        gain = [kt(f"gain{r}", [P, 4, D], F32) for r in range(2)]
        HALF = (slice(0, 2), slice(2, 4))

        permute_words(0, 0)
        permute_words(0, 1)
        nc.vector.tensor_scalar_min(out=am[:], in0=al[:], scalar1=40.0)
        nc.scalar.activation(out=ex[:], in_=am[:], func=ACT.Exp)
        permute_words(0, 2)
        permute_words(0, 3)
        permute_scales()
        permute_words(1, 0)
        permute_words(1, 1)
        for s in HALF:
            nc.scalar.activation(out=ex[:, s], in_=ex[:, s], func=ACT.Ln, bias=1.0)
        for s in HALF:
            nc.vector.tensor_tensor(out=sp[:, s], in0=ex[:, s], in1=al[:, s], op=ALU.max)
        for g in range(2):
            interleave_v(0, g, nc.scalar.copy)
        for s in HALF:
            nc.scalar.activation(out=den[:, s], in_=sp[:, s], func=ACT.Square)
        for t in range(4):
            nc.scalar.activation(out=den[:, t], in_=den[:, t], func=ACT.Ln, bias=w2[:, t : t + 1])
        for s in HALF:
            nc.scalar.activation(out=inv[:, s], in_=den[:, s], func=ACT.Exp, scale=-1.0)
        permute_words(1, 2)
        quantize_v(0)
        permute_words(1, 3)
        vi[1] = vi_tile(1)
        for g in range(2):
            interleave_v(1, g, gpsimd_copy)

        cr, ci, st, zt, zq, zs, ob = {}, {}, {}, {}, {}, {}, {}
        of = [kt(f"of{b}", [P, 2, 4, D], F32) for b in range(B)]
        oq = [kt(f"oq{b}", [P, 2, D], U32) for b in range(B)]
        osc = kt("osc", [P, 2, 1024], U8)

        def weight(i, g, r, t):
            return (
                words[i][:, g, r, t].bitcast(FP4X4),
                scales[i][:, 2 * g + r, t],
            )

        def product(i, bank, r, rhs, rhs_scale):
            for t in range(4):
                for g in range(2):
                    lhs, lhs_scale = weight(i, g, r, t)
                    nc.tensor.matmul_mx(
                        out=bank[:, t, :],
                        lhsT=lhs,
                        lhsT_scale=lhs_scale,
                        rhs=rhs(g),
                        rhs_scale=rhs_scale(g),
                        start=(g == 0),
                        stop=(g == 1),
                    )

        def stage1(u):
            b, h = UNITS[u]
            sl = slice(h * H, (h + 1) * H)
            cr[u] = ps.tile([P, 4, H], F32, name="cr")
            ci[u] = ps.tile([P, 4, H], F32, name="ci")
            for r, bank in ((0, cr[u]), (1, ci[u])):
                product(0, bank, r, lambda g: vq[b][:, g, sl].bitcast(FP8X4), lambda g: vs[b][:, g, sl])

        def combine(u):
            h = UNITS[u][1]
            sl = slice(h * H, (h + 1) * H)
            st[u, 0] = wt("s0", [P, 4, H], F32)
            st[u, 1] = wt("s1", [P, 4, H], F32)
            for r, bank in ((0, cr[u]), (1, ci[u])):
                nc.vector.tensor_tensor(out=st[u, r][:], in0=bank[:], in1=sp[:, :, sl], op=ALU.mult)
            for r, bank, coeff in ((0, ci[u], w32), (1, cr[u], wn)):
                s = st[u, r]
                for t in range(4):
                    nc.vector.scalar_tensor_tensor(
                        out=s[:, t],
                        in0=bank[:, t],
                        scalar=coeff[:, t : t + 1],
                        in1=s[:, t],
                        op0=ALU.mult,
                        op1=ALU.add,
                    )

        def gain_z(u, r, engine):
            h = UNITS[u][1]
            sl = slice(h * H, (h + 1) * H)
            if r == 0:
                zt[u] = wt("zt", [P, 2, H, 4], BF16, bufs=1)
            engine.tensor_tensor(
                out=zt[u][:, r].rearrange("p (c i) t -> p c t i", i=4),
                in0=st[u, r][:].rearrange("p t (c i) -> p c t i", i=4),
                in1=gain[r][:, :, sl].rearrange("p t (c i) -> p c t i", i=4),
                op=ALU.mult,
            )

        def quantize_z(u):
            zq[u] = wt("zq", [P, 2, H], U32)
            zs[u] = wt("zs", [P, 2, H], U8)
            nc.vector.quantize_mx(
                out=zq[u][:].rearrange("p g c -> p (g c)").bitcast(FP8X4),
                scales=zs[u][:].rearrange("p g c -> p (g c)"),
                in_=zt[u][:].rearrange("p g c t -> p (g c t)"),
            )

        def quantize_out_half(u, r):
            b, h = UNITS[u]
            nc.vector.quantize_mx(
                out=oq[b][:, r, h * H : (h + 1) * H].bitcast(FP8X4),
                scales=osc[:, r, b * D + h * H : b * D + (h + 1) * H],
                in_=ob[u][:, r].rearrange("p c t -> p (c t)"),
            )

        def finish(u):
            b, h = UNITS[u]
            sl = slice(h * H, (h + 1) * H)
            for r in range(2):
                nc.vector.tensor_copy(
                    out=ob[u][:, r].rearrange("p (c i) t -> p c t i", i=4),
                    in_=of[b][:, r, :, sl].rearrange("p t (c i) -> p c t i", i=4),
                )
                quantize_out_half(u, r)

        def stage2(u):
            b, h = UNITS[u]
            sl = slice(h * H, (h + 1) * H)
            ob[u] = wt("ob", [P, 2, H, 4], BF16, bufs=3)
            for r in range(2):
                bank = ps.tile([P, 4, H], F32, name=f"o{r}")
                product(1, bank, r, lambda g: zq[u][:, g].bitcast(FP8X4), lambda g: zs[u][:, g])
                nc.scalar.copy(out=of[b][:, r, :, sl], in_=bank[:])
                if u < len(UNITS) - 2:
                    nc.scalar.copy(out=ob[u][:, r], in_=bank[:].rearrange("p t c -> p c t"))

        out_words = out_1.rearrange("g p m t -> g p (m t)").bitcast(I32).rearrange("g p m -> p g m")
        out_scales = out_2.bitcast(I32)

        def store(u):
            b, h = UNITS[u]
            if b < 2:
                if h == 1:
                    nc.sync.dma_start(
                        out=out_0[b].rearrange("(g p t) d -> p g (t d)", g=2, t=4),
                        in_=of[b][:].rearrange("p g t d -> p g (t d)"),
                    )
            else:
                sl = slice(h * H, (h + 1) * H)
                for g in range(2):
                    nc.sync.dma_start(
                        out=out_0[b, 512 * g : 512 * (g + 1), sl].rearrange("(p t) d -> p t d", t=4),
                        in_=of[b][:, g, :, sl],
                    )

        def store_planes(u):
            b, h = UNITS[u]
            if h == 1:
                nc.sync.dma_start(out=out_words[:, :, b * D : (b + 1) * D], in_=oq[b][:].bitcast(I32))
            if (b, h) == (2, 1) or (b, h) == (3, 1):
                lo, hi = (0, 192) if b == 2 else (192, 256)
                for q in range(4):
                    nc.sync.dma_start(
                        out=out_scales[:, 4 * q : 4 * q + 4, lo:hi].rearrange("g q n -> q g n"),
                        in_=osc[32 * q : 32 * q + 4, :, :].bitcast(I32)[:, :, lo:hi],
                    )

        n = len(UNITS)
        stage1(0)
        for k in range(n + 1):
            if k + 1 < n:
                stage1(k + 1)
            if k < n:
                combine(k)
            if k == 0:
                quantize_v(1)
                for r in (1, 0):
                    for s in HALF:
                        nc.vector.tensor_tensor(out=gain[r][:, s], in0=be[:, r, s], in1=inv[:, s], op=ALU.mult)
                for b in (2, 3):
                    for g in range(2):
                        interleave_v(b, g, nc.scalar.copy)
            if k in (2, 4):
                quantize_v(k // 2 + 1)
            if k >= 3:
                for r in range(2):
                    quantize_out_half(k - 3, r)
                store_planes(k - 3)
            if k >= 2:
                store(k - 2)
            if k >= 1:
                for r in range(2):
                    gain_z(k - 1, r, nc.vector if k == n else nc.gpsimd)
                quantize_z(k - 1)
                stage2(k - 1)
        finish(n - 2)
        store_planes(n - 2)
        store(n - 1)
        finish(n - 1)
        store_planes(n - 1)
